import numpy as np
import ml_dtypes


def mxq(x, axis, fmt="e4m3"):
    dtype, down = {"e4m3": (ml_dtypes.float8_e4m3fn, 7), "e5m2": (ml_dtypes.float8_e5m2, 14)}[fmt]
    v = np.moveaxis(np.asarray(x, np.float32).astype(ml_dtypes.bfloat16).astype(np.float64), axis, -1)
    blocks = v.reshape(v.shape[:-1] + (-1, 32))
    amax = np.abs(blocks).max(-1, keepdims=True)
    byte = np.maximum(np.where(amax > 0, np.frexp(amax)[1] - 1 + 127, 0) - down, 1)
    scale = np.exp2(byte - 127.0)
    codes = (blocks / scale).astype(np.float32).astype(dtype).astype(np.float64)
    return np.moveaxis((codes * scale).reshape(v.shape), -1, axis)


WIDE = False


def mx_kscale(k):
    if not WIDE:
        return np.ones(k)
    levels = np.array([30, -30])
    if k % 512:
        return np.exp2(np.random.permutation(np.resize(levels, k // 32))).repeat(32)
    a = np.empty((k // 512, 16))
    for p in range(k // 512):
        a[p, :8] = np.random.permutation(np.resize(levels, 8))
        for g in range(8):
            far = levels[np.abs(levels - a[p, g]) >= 10]
            a[p, g + 8] = far[np.random.randint(len(far))]
    return np.exp2(a.ravel()).repeat(32)


BF16 = ml_dtypes.bfloat16


def bf(x):
    return np.asarray(x, np.float32).astype(BF16)


def f64(x):
    return np.asarray(x).astype(np.float64)


E2M1 = np.array([0.0, 0.5, 1.0, 1.5, 2.0, 3.0, 4.0, 6.0, -0.0, -0.5, -1.0, -1.5, -2.0, -3.0, -4.0, -6.0])


def pack_weight(w, fmt):
    k, n = w.shape
    w = f64(bf(w)).reshape(k // 32, 32, n)
    amax = np.abs(w).max(1)
    if fmt in ("e4m3", "e5m2"):
        byte = np.frexp(amax)[1] - 1 + 127 - (7 if fmt == "e4m3" else 14)
    else:
        mant, ex = np.frexp(amax / 6.0)
        byte = np.where(mant > 0.5, ex, ex - 1) + 127
    byte = np.clip(np.where(amax > 0, byte, 1), 1, 254)
    scaled = (w * np.exp2(127.0 - byte)[:, None, :]).reshape(k, n).astype(np.float32)
    by_word = np.ascontiguousarray(scaled.reshape(k // 512, 128, 4, n).transpose(0, 1, 3, 2))
    if fmt in ("e4m3", "e5m2"):
        words = by_word.astype(ml_dtypes.float8_e4m3fn if fmt == "e4m3" else ml_dtypes.float8_e5m2).view(np.uint8)
    else:
        c = by_word.astype(ml_dtypes.float4_e2m1fn).view(np.uint8) & 0xF
        words = c[..., 0::2] | (c[..., 1::2] << 4)
    return np.ascontiguousarray(words), np.ascontiguousarray(byte.astype(np.uint8).reshape(k // 512, 16, n))


def unpack_weight(words, scales, fmt):
    g, p, n, _ = words.shape
    if fmt in ("e4m3", "e5m2"):
        vals = np.ascontiguousarray(words).view(ml_dtypes.float8_e4m3fn if fmt == "e4m3" else ml_dtypes.float8_e5m2).astype(np.float64)
    else:
        nib = np.empty((g, p, n, 4), np.uint8)
        nib[..., 0::2] = words & 0xF
        nib[..., 1::2] = words >> 4
        vals = E2M1[nib]
    vals = vals * np.repeat(np.exp2(scales.astype(np.float64) - 127.0), 8, axis=1)[..., None]
    return vals.transpose(0, 1, 3, 2).reshape(g * 512, n)


M, K, U = 2048, 1024, 512


def setup_inputs():
    s = mx_kscale(K)
    G = np.random.standard_normal((K, M)) * np.exp(0.5 * np.random.standard_normal((K, M)))
    lam_words, lam_scales = pack_weight(G * s[:, None], "e5m2")
    return {"lam_words": lam_words,
            "lam_scales": lam_scales,
            "a": bf(np.random.standard_normal((K, K)) / np.sqrt(K) / s[:, None]),
            "b": bf(np.random.standard_normal((K, U)) / np.sqrt(K) / s[:, None]),
            "dx": bf(np.random.standard_normal((M, K))),
            "du": bf(np.random.standard_normal((M, U))),
            "x_cost": bf(np.exp(0.5 * np.random.standard_normal(K))),
            "u_cost": bf(np.exp(0.5 * np.random.standard_normal(U)))}


def reference(lam_words, lam_scales, a, b, dx, du, x_cost, u_cost):
    lam = unpack_weight(lam_words, lam_scales, "e5m2")
    back = lam.T @ mxq(f64(a), 0, "e4m3")
    ctrl = lam.T @ mxq(f64(b), 0, "e4m3")
    costate = back + f64(dx) * f64(x_cost)
    grad_u = ctrl + f64(du) * f64(u_cost)
    return costate, grad_u

from contextlib import ExitStack

import concourse.mybir as mybir
from concourse.masks import make_identity

M, K, U = 2048, 1024, 512
FLOPS = 2 * M * K * (K + U)

F32 = mybir.dt.float32
BF16 = mybir.dt.bfloat16
I32 = mybir.dt.int32
U32 = mybir.dt.uint32
U8 = mybir.dt.uint8
E4M3X4 = mybir.dt.float8_e4m3fn_x4
E5M2X4 = mybir.dt.float8_e5m2_x4
MULT = mybir.AluOpType.mult
ADD = mybir.AluOpType.add

P = 128
PACK = 4
K_PASS = P * PACK
PASSES = K // K_PASS
N_TILE = 512
M_TILES = M // P
LAM_HEAD = 512


def tile_costate_backward_step_e1_kernel(
    tc, lam_words, lam_scales, a, b, dx, du, x_cost, u_cost, out_0, out_1
):
    nc = tc.nc
    with ExitStack() as ctx:
        keep = ctx.enter_context(tc.tile_pool(name="keep", bufs=1))
        stage = ctx.enter_context(tc.tile_pool(name="stage", bufs=2))
        psum = ctx.enter_context(tc.psum_pool(name="psum", bufs=1))
        ctx.enter_context(tc.manual_schedule())

        cost_rows = keep.tile([P, P], BF16, name="cost_rows")
        cost_cols = keep.tile([P, 16], BF16, name="cost_cols")
        ident = keep.tile([P, P], BF16, name="ident")
        x_cost_sb = keep.tile([P, 2, K], BF16, name="x_cost_sb")
        lam_plane = keep.tile([P, PASSES, M], U8, name="lam_plane", align_bytes=64)
        lam_head = keep.tile([P, PASSES, LAM_HEAD], U32, name="lam_head", align_bytes=64)
        lam_rest = keep.tile([P, PASSES, M - LAM_HEAD], U32, name="lam_rest", align_bytes=64)
        a_raw = [keep.tile([P, PACK, K], BF16, name="a_raw%d" % g) for g in range(PASSES)]
        b_raw = [keep.tile([P, PACK, U], BF16, name="b_raw%d" % g) for g in range(PASSES)]
        dx_sb = [keep.tile([P, 2, K], BF16, name="dx_sb%d" % j) for j in range(M_TILES // 2)]
        du_sb = [keep.tile([P, 4, U], BF16, name="du_sb%d" % j) for j in range(M_TILES // 4)]
        costate = [keep.tile([P, 2, K], F32, name="costate%d" % j) for j in range(M_TILES // 2)]
        grad_u = [keep.tile([P, 2, U], F32, name="grad_u%d" % j) for j in range(M_TILES // 2)]
        w_codes = {}
        w_scales = {}
        for g in range(PASSES):
            for n in range(3):
                w_codes[g, n] = keep.tile([P, N_TILE], U32, name="w_codes%d%d" % (g, n), align_bytes=64)
                w_scales[g, n] = keep.tile([P, N_TILE], U8, name="w_scales%d%d" % (g, n), align_bytes=64)

        nc.vector.memset(cost_rows[:], 0.0)
        nc.vector.memset(lam_plane[:].rearrange("p g m -> p (g m)").bitcast(I32), 0)
        nc.scalar.dma_start(out=cost_rows[0:8, :], in_=x_cost.rearrange("(c r) -> c r", r=P))
        nc.scalar.dma_start(out=cost_rows[8:12, :], in_=u_cost.rearrange("(c r) -> c r", r=P))
        make_identity(nc, ident[:])
        scale_words = lam_scales.bitcast(I32).rearrange("g (q r) w -> r q g w", r=4)
        for r in range(4):
            nc.gpsimd.dma_start(out=lam_plane[r:P:32, :, :].bitcast(I32), in_=scale_words[r])

        lam_i32 = lam_words.rearrange("g p m t -> p g (m t)").bitcast(I32)

        def load_dx(j):
            nc.sync.dma_start(out=dx_sb[j][:], in_=dx[2 * P * j : 2 * P * (j + 1), :].rearrange("(e p) n -> p e n", p=P))

        def load_du(j):
            nc.sync.dma_start(out=du_sb[j][:], in_=du[4 * P * j : 4 * P * (j + 1), :].rearrange("(e p) n -> p e n", p=P))

        for g in range(PASSES):
            nc.sync.dma_start(out=a_raw[g][:], in_=a[K_PASS * g : K_PASS * (g + 1), :].rearrange("(p t) n -> p t n", t=PACK))
        for g in range(PASSES):
            nc.sync.dma_start(out=b_raw[g][:], in_=b[K_PASS * g : K_PASS * (g + 1), :].rearrange("(p t) n -> p t n", t=PACK))
        nc.sync.dma_start(out=lam_head[:].bitcast(I32), in_=lam_i32[:, :, 0:LAM_HEAD])
        load_dx(0)
        load_du(0)
        load_dx(1)
        nc.sync.dma_start(out=lam_rest[:].bitcast(I32), in_=lam_i32[:, :, LAM_HEAD:M])
        for j in range(1, M_TILES // 4):
            load_dx(2 * j)
            load_du(j)
            load_dx(2 * j + 1)

        grouped = {}

        def interleave(g, n, on_vector):
            raw = a_raw[g][:, :, N_TILE * n : N_TILE * (n + 1)] if n < 2 else b_raw[g][:]
            tag = "grouped_v" if on_vector else "grouped_s"
            dst = stage.tile([P, N_TILE, PACK], BF16, name=tag, tag=tag, align_bytes=64)
            grouped[g, n] = dst
            o = dst[:].rearrange("p (c i) t -> p c t i", i=4)
            s = raw.rearrange("p t (c i) -> p c t i", i=4)
            if on_vector:
                nc.vector.tensor_copy(out=o, in_=s)
            else:
                nc.scalar.copy(out=o, in_=s)

        def quantize(g, n):
            nc.vector.quantize_mx(
                out=w_codes[g, n][:].bitcast(E4M3X4),
                scales=w_scales[g, n][:],
                in_=grouped[g, n][:].rearrange("p w t -> p (w t)"),
            )

        interleave(0, 0, True)
        interleave(0, 1, False)
        quantize(0, 0)
        interleave(1, 0, True)
        interleave(1, 1, False)
        turned = psum.tile([P, P], BF16, name="turned", tag="acc", bufs=6)
        nc.tensor.transpose(turned[:], cost_rows[:], ident[:])
        nc.vector.tensor_copy(out=cost_cols[:], in_=turned[:, 0:16])
        x_cost_ps = psum.tile([P, K], BF16, name="x_cost_ps")
        u_cost_ps = psum.tile([P, U], BF16, name="u_cost_ps")
        for c in range(K // P):
            nc.tensor.transpose(x_cost_ps[:, P * c : P * (c + 1)], cost_cols[:, c : c + 1].to_broadcast([P, P]), ident[:])
        for c in range(U // P):
            nc.tensor.transpose(u_cost_ps[:, P * c : P * (c + 1)], cost_cols[:, 8 + c : 9 + c].to_broadcast([P, P]), ident[:])

        quantize(0, 1)
        quantize(1, 0)
        interleave(0, 2, False)
        nc.scalar.copy(out=x_cost_sb[:, 1, :], in_=x_cost_ps[:])
        nc.scalar.copy(out=x_cost_sb[:, 0, :], in_=x_cost_ps[:])
        interleave(1, 2, True)
        quantize(1, 1)
        quantize(1, 2)
        quantize(0, 2)

        def x_product(j, lo, hi):
            nc.gpsimd.tensor_tensor(
                out=costate[j][:, lo:hi, :].rearrange("p e n -> p (e n)"),
                in0=dx_sb[j][:, lo:hi, :].rearrange("p e n -> p (e n)"),
                in1=x_cost_sb[:, lo:hi, :].rearrange("p e n -> p (e n)"),
                op=MULT,
            )

        def u_product(i):
            nc.vector.tensor_tensor(out=grad_u[i // 2][:, i % 2, :], in0=du_sb[i // 4][:, i % 4, :], in1=u_cost_ps[:], op=MULT)

        nc.vector.tensor_tensor(out=costate[0][:, 0, :], in0=dx_sb[0][:, 0, :], in1=x_cost_ps[:], op=MULT)
        u_product(0)
        x_product(0, 1, 2)
        for i in range(M_TILES):
            j, e = divmod(i, 2)
            if e == 0 and j + 1 < M_TILES // 2:
                x_product(j + 1, 0, 2)
            m0 = P * i
            lam, c0 = (lam_head, m0) if m0 < LAM_HEAD else (lam_rest, m0 - LAM_HEAD)
            for n in range(3):
                acc = psum.tile([P, N_TILE], F32, name="acc", tag="acc", bufs=6)
                for g in range(PASSES):
                    nc.tensor.matmul_mx(
                        out=acc[:],
                        lhsT=lam[:, g, c0 : c0 + P].bitcast(E5M2X4),
                        lhsT_scale=lam_plane[:, g, m0 : m0 + P],
                        rhs=w_codes[g, n][:].bitcast(E4M3X4),
                        rhs_scale=w_scales[g, n][:],
                        start=(g == 0),
                        stop=(g == PASSES - 1),
                    )
                res = costate[j][:, e, N_TILE * n : N_TILE * (n + 1)] if n < 2 else grad_u[j][:, e, :]
                nc.vector.tensor_tensor(out=res, in0=acc[:], in1=res, op=ADD)
                if n == 1:
                    nc.sync.dma_start(out=out_0[m0 : m0 + P, :], in_=costate[j][:, e, :])
            if i + 1 < M_TILES:
                u_product(i + 1)
            if e == 1:
                nc.sync.dma_start(
                    out=out_1[2 * P * j : 2 * P * (j + 1), :].rearrange("(e p) n -> p e n", p=P), in_=grad_u[j][:]
                )
